import numpy as np
import ml_dtypes


def mxq(x, axis, fmt="e4m3"):
    dtype, down = {"e4m3": (ml_dtypes.float8_e4m3fn, 7), "e5m2": (ml_dtypes.float8_e5m2, 14)}[fmt]
    v = np.moveaxis(np.asarray(x, np.float32).astype(ml_dtypes.bfloat16).astype(np.float64), axis, -1)
    blocks = v.reshape(v.shape[:-1] + (-1, 32))
    amax = np.abs(blocks).max(-1, keepdims=True)
    byte = np.maximum(np.where(amax > 0, np.frexp(amax)[1] - 1 + 127, 0) - down, 1)
    scale = np.exp2(byte - 127.0)
    codes = (blocks / scale).astype(np.float32).astype(dtype).astype(np.float64)
    return np.moveaxis((codes * scale).reshape(v.shape), -1, axis)


WIDE = False


def mx_kscale(k):
    if not WIDE:
        return np.ones(k)
    levels = np.array([10, -10, 5, -5, 0])
    if k % 512:
        return np.exp2(np.random.permutation(np.resize(levels, k // 32))).repeat(32)
    a = np.empty((k // 512, 16))
    for p in range(k // 512):
        a[p, :8] = np.random.permutation(np.resize(levels, 8))
        for g in range(8):
            far = levels[np.abs(levels - a[p, g]) >= 10]
            a[p, g + 8] = far[np.random.randint(len(far))]
    return np.exp2(a.ravel()).repeat(32)


BF16 = ml_dtypes.bfloat16


def bf(x):
    return np.asarray(x, np.float32).astype(BF16)


def f64(x):
    return np.asarray(x).astype(np.float64)


E2M1 = np.array([0.0, 0.5, 1.0, 1.5, 2.0, 3.0, 4.0, 6.0, -0.0, -0.5, -1.0, -1.5, -2.0, -3.0, -4.0, -6.0])


def pack_weight(w, fmt):
    k, n = w.shape
    w = f64(bf(w)).reshape(k // 32, 32, n)
    amax = np.abs(w).max(1)
    if fmt == "e4m3":
        byte = np.frexp(amax)[1] - 1 + 127 - 7
    else:
        mant, ex = np.frexp(amax / 6.0)
        byte = np.where(mant > 0.5, ex, ex - 1) + 127
    byte = np.clip(np.where(amax > 0, byte, 1), 1, 254)
    scaled = (w * np.exp2(127.0 - byte)[:, None, :]).reshape(k, n).astype(np.float32)
    by_word = np.ascontiguousarray(scaled.reshape(k // 512, 128, 4, n).transpose(0, 1, 3, 2))
    if fmt == "e4m3":
        words = by_word.astype(ml_dtypes.float8_e4m3fn).view(np.uint8)
    else:
        c = by_word.astype(ml_dtypes.float4_e2m1fn).view(np.uint8) & 0xF
        words = c[..., 0::2] | (c[..., 1::2] << 4)
    return np.ascontiguousarray(words), np.ascontiguousarray(byte.astype(np.uint8).reshape(k // 512, 16, n))


def unpack_weight(words, scales, fmt):
    g, p, n, _ = words.shape
    if fmt == "e4m3":
        vals = np.ascontiguousarray(words).view(ml_dtypes.float8_e4m3fn).astype(np.float64)
    else:
        nib = np.empty((g, p, n, 4), np.uint8)
        nib[..., 0::2] = words & 0xF
        nib[..., 1::2] = words >> 4
        vals = E2M1[nib]
    vals = vals * np.repeat(np.exp2(scales.astype(np.float64) - 127.0), 8, axis=1)[..., None]
    return vals.transpose(0, 1, 3, 2).reshape(g * 512, n)
def pack4(w):
    words, scales = pack_weight(w, "e2m1")
    return words.reshape(words.shape[0], 128, -1), scales


def unpack4(words, scales):
    return unpack_weight(words.reshape(words.shape[0], 128, -1, 2), scales, "e2m1")


def planes(Y):
    n, m = Y.shape
    b = f64(bf(Y)).reshape(n // 32, 32, m)
    amax = np.abs(b).max(1)
    byte = np.clip(np.where(amax > 0, np.frexp(amax)[1] - 1 + 127 - 7, 1), 1, 254)
    codes = (b * np.exp2(127.0 - byte)[:, None, :]).reshape(n, m).astype(np.float32).astype(ml_dtypes.float8_e4m3fn).view(np.uint8)
    words = codes.reshape(n // 512, 128, 4, m).transpose(0, 1, 3, 2)
    return np.ascontiguousarray(words), np.ascontiguousarray(byte.astype(np.uint8).reshape(n // 512, 16, m))


S, K, F, N = 1024, 1024, 2048, 1024
CLAIM_SIZE = 3.0
CAP_LOW = 0.3
SPREAD = 0.8

def setup_inputs():
    s = mx_kscale(K)
    t = mx_kscale(F)
    grades = np.random.rand(S, K) ** 3
    claims = np.random.randn(K, F) * CLAIM_SIZE / np.sqrt(K)
    recovery = np.random.randn(F, N) / np.sqrt(F)
    claims_words, claims_scales = pack4(claims / s[:, None] * t[None, :])
    recovery_words, recovery_scales = pack4(recovery / t[:, None])
    return {
        "default_grades": bf(grades * s[None, :]),
        "claims_words": claims_words,
        "claims_scales": claims_scales,
        "loss_cap": bf((CAP_LOW + np.random.rand(F)) * t),
        "recovery_words": recovery_words,
        "recovery_scales": recovery_scales,
        "scenario_scale": bf(np.exp(0.3 * np.random.randn(S))),
        "other_result": bf(0.4 * np.random.randn(N)),
        "gearing": bf(np.exp(SPREAD * np.random.randn(N))),
    }

def reference(default_grades, claims_words, claims_scales, loss_cap, recovery_words, recovery_scales, scenario_scale, other_result, gearing):
    C = unpack4(claims_words, claims_scales)
    R = unpack4(recovery_words, recovery_scales)
    loss = mxq(f64(default_grades), 1, "e4m3") @ C
    capped = np.minimum(loss, f64(loss_cap)[None, :])
    passed = mxq(capped, 1, "e4m3") @ R
    y = (passed * f64(scenario_scale)[:, None] + f64(other_result)[None, :]) * f64(gearing)[None, :]
    words, scales = planes(y.T)
    return y, words, scales

@@ -1,0 +1,388 @@
+from contextlib import ExitStack
+
+import concourse.mybir as mybir
+from concourse.masks import make_identity
+
+S, K, F, N = 1024, 1024, 2048, 1024
+FLOPS = 2 * S * K * F + 2 * S * F * N
+
+F32 = mybir.dt.float32
+BF16 = mybir.dt.bfloat16
+I32 = mybir.dt.int32
+U32 = mybir.dt.uint32
+U8 = mybir.dt.uint8
+FP8X4 = mybir.dt.float8_e4m3fn_x4
+FP4X4 = mybir.dt.float4_e2m1fn_x4
+ALU = mybir.AluOpType
+
+P = 128
+PASS = 512
+TILES = S // P
+KG, FG, NG = K // PASS, F // PASS, N // PASS
+RING = 4
+
+
+def tile_capped_interbank_loss_planes_h1_kernel(
+    tc, default_grades, claims_words, claims_scales, loss_cap, recovery_words, recovery_scales,
+    scenario_scale, other_result, gearing, out_0, out_1, out_2,
+):
+    nc = tc.nc
+    with ExitStack() as ctx:
+        keep = ctx.enter_context(tc.tile_pool(name="keep", bufs=1))
+        work = ctx.enter_context(tc.tile_pool(name="work", bufs=3))
+        psum = ctx.enter_context(tc.psum_pool(name="psum", bufs=1))
+        ctx.enter_context(tc.manual_schedule())
+
+        used = []
+
+        def mm_bank():
+            n = len([x for x in used if x == "mm"])
+            used.append("mm")
+            return psum.tile([P, PASS], F32, name="mm%d" % (n % RING))
+
+        def tp_bank():
+            n = len([x for x in used if x == "tp"])
+            used.append("tp")
+            return psum.tile([P, 4, P], F32, name="tp%d" % (n % RING))
+
+        c_scales = keep.tile([P, KG, F], U8, align_bytes=64)
+        r_scales = keep.tile([P, FG, N], U8, align_bytes=64)
+        ident = keep.tile([P, P], F32)
+
+        d_raw = [None] + [keep.tile([P, K], BF16, name="d_raw%d" % i, align_bytes=64) for i in range(1, TILES)]
+        c_codes = [keep.tile([P, KG, 2 * PASS], U8, name="c_codes%d" % fb, align_bytes=64) for fb in range(FG)]
+        r_codes = [keep.tile([P, FG, 2 * PASS], U8, name="r_codes%d" % nb, align_bytes=64) for nb in range(NG)]
+        d_first = [keep.tile([P, PASS], BF16, name="d_first%d" % g, align_bytes=64) for g in range(KG)]
+        cap_col = keep.tile([P, 16], BF16)
+        other_col = keep.tile([P, 8], BF16)
+        gear_col = keep.tile([P, 8], BF16)
+        ss_rows = keep.tile([TILES, P], BF16)
+        ss_stage = keep.tile([P, P], F32)
+
+        def load_d(i):
+            nc.sync.dma_start(out=d_raw[i][:], in_=default_grades[i * P:(i + 1) * P, :])
+
+        def load_scales(plane, scales):
+            words = scales.bitcast(I32)
+            for q in range(4):
+                nc.sync.dma_start(
+                    out=plane[32 * q:32 * q + 4, :, :].bitcast(I32),
+                    in_=words[:, 4 * q:4 * q + 4, :].rearrange("g r c -> r g c"),
+                )
+
+        def load_codes(tile, words, b):
+            words = words.bitcast(I32).rearrange("g p c -> p g c")
+            nc.sync.dma_start(out=tile[:].bitcast(I32), in_=words[:, :, b * 256:(b + 1) * 256])
+
+        nc.vector.memset(c_scales[:].bitcast(I32), 0)
+        nc.vector.memset(r_scales[:].bitcast(I32), 0)
+        nc.vector.memset(ss_stage[:], 0.0)
+        nc.gpsimd.dma_start(out=cap_col[:], in_=loss_cap.rearrange("(p c) -> p c", p=P))
+        make_identity(nc, ident[:])
+        nc.gpsimd.dma_start(out=other_col[:], in_=other_result.rearrange("(p c) -> p c", p=P))
+        nc.gpsimd.dma_start(out=gear_col[:], in_=gearing.rearrange("(p c) -> p c", p=P))
+        nc.gpsimd.dma_start(out=ss_rows[:], in_=scenario_scale.rearrange("(i p) -> i p", p=P))
+        for g in range(KG):
+            nc.sync.dma_start(out=d_first[g][:], in_=default_grades[0:P, g * PASS:(g + 1) * PASS])
+        load_codes(c_codes[0], claims_words, 0)
+        load_scales(c_scales, claims_scales)
+        load_codes(c_codes[1], claims_words, 1)
+        load_d(1)
+        load_codes(c_codes[2], claims_words, 2)
+        load_codes(c_codes[3], claims_words, 3)
+        load_d(2)
+        load_scales(r_scales, recovery_scales)
+        for nb in range(NG):
+            load_codes(r_codes[nb], recovery_words, nb)
+        for i in range(3, TILES):
+            load_d(i)
+
+        cap_all = keep.tile([P, FG, PASS], BF16)
+        other_all = keep.tile([P, N], BF16)
+        gear_all = keep.tile([P, N], BF16)
+        ss_col = keep.tile([P, TILES], F32)
+        y_scales = keep.tile([P, NG, S], U8, align_bytes=64)
+
+        def spread_cap():
+            words = cap_col[:].bitcast(F32)
+            dest = cap_all[:].bitcast(F32).rearrange("m g (u h l) -> m g u h l", u=2, l=4)
+            for u in range(2):
+                bank = tp_bank()
+                for l in range(4):
+                    c = 2 * l + u
+                    nc.tensor.transpose(bank[:, l, :], words[:, c:c + 1].to_broadcast([P, P]), ident[:])
+                copy = nc.vector.tensor_copy if u == 0 else nc.scalar.copy
+                copy(out=dest[:, :, u, :, :], in_=bank[:].rearrange("m l (g h) -> m g h l", g=FG))
+
+        def spread_row(col, dest):
+            words = col[:].bitcast(F32)
+            bank = tp_bank()
+            for c in range(4):
+                nc.tensor.transpose(bank[:, c, :], words[:, c:c + 1].to_broadcast([P, P]), ident[:])
+            nc.scalar.copy(out=dest[:].bitcast(F32).rearrange("m (p c) -> m p c", c=4), in_=bank[:].rearrange("m c p -> m p c"))
+
+        def turn_ss():
+            nc.scalar.copy(out=ss_stage[0:TILES, :], in_=ss_rows[:])
+            bank = tp_bank()
+            nc.tensor.transpose(bank[:, 0, :], ss_stage[:], ident[:])
+            nc.scalar.copy(out=ss_col[:], in_=bank[:, 0, 0:TILES])
+
+        d_sorted, d_turned, d_q = {}, {}, {}
+        h_rows, h_turned, h_q = {}, {}, {}
+        z_part, y_f32, y_rows, y_turned = {}, {}, {}, {}
+
+        def leave_bank(bank, name):
+            turned = work.tile([P, 1024], BF16, name=name, align_bytes=64)
+            nc.scalar.copy(
+                out=turned[:].bitcast(F32).rearrange("p (g s u) -> p g s u", g=2, u=2),
+                in_=bank[:].rearrange("p (g u) s -> p g s u", u=2),
+            )
+            return turned
+
+        def sort_d(i):
+            srt = work.tile([P, K // 2], F32, name="d_sorted")
+            nc.scalar.copy(
+                out=srt[:].rearrange("s (g u j) -> s g u j", g=KG, u=2),
+                in_=d_raw[i][:].bitcast(F32).rearrange("s (g j u) -> s g u j", g=KG, u=2),
+            )
+            d_sorted[i] = srt
+
+        def turn_d(i):
+            bank = tp_bank()
+            for g in range(KG):
+                for u in range(2):
+                    if i in d_sorted:
+                        src = d_sorted[i][:, (2 * g + u) * P:(2 * g + u + 1) * P]
+                    else:
+                        src = d_raw[i][:].bitcast(F32)[:, 256 * g + u:256 * (g + 1):2]
+                    nc.tensor.transpose(bank[:, 2 * g + u, :], src, ident[:])
+            return bank
+
+        def quantize(turned, name):
+            codes = work.tile([P, 256], U32, name=name + "_codes", align_bytes=64)
+            scales = work.tile([P, 256], U8, name=name + "_scales", align_bytes=64)
+            nc.vector.quantize_mx(out=codes[:].bitcast(FP8X4), scales=scales[:], in_=turned[:])
+            return codes, scales
+
+        def mm1(i, fb):
+            bank = mm_bank()
+            for g in range(KG):
+                codes, scales = d_q[(i, g)]
+                nc.tensor.matmul_mx(
+                    out=bank[:],
+                    lhsT=codes.bitcast(FP8X4),
+                    lhsT_scale=scales,
+                    rhs=c_codes[fb][:, g, :].bitcast(FP4X4),
+                    rhs_scale=c_scales[:, g, fb * PASS:(fb + 1) * PASS],
+                    start=(g == 0), stop=(g == KG - 1),
+                )
+            rows = work.tile([P, PASS], BF16, name="h_rows%d" % fb, align_bytes=64)
+            nc.vector.tensor_tensor(
+                out=rows[:].rearrange("s (u j e) -> s u j e", u=2, e=2),
+                in0=bank[:].rearrange("s (j u e) -> s u j e", u=2, e=2),
+                in1=cap_all[:, fb, :].rearrange("s (u j e) -> s u j e", u=2, e=2),
+                op=ALU.min,
+            )
+            h_rows[(i, fb)] = rows
+
+        def turn_pair(rows_a, rows_b):
+            bank = tp_bank()
+            for g, rows in enumerate((rows_a, rows_b)):
+                for u in range(2):
+                    nc.tensor.transpose(bank[:, 2 * g + u, :], rows[:].bitcast(F32)[:, u * P:(u + 1) * P], ident[:])
+            return bank
+
+        def mm2(i, nb):
+            bank = mm_bank()
+            for g in range(FG):
+                codes, scales = h_q[(i, g // 2)]
+                cols = slice((g % 2) * P, (g % 2 + 1) * P)
+                nc.tensor.matmul_mx(
+                    out=bank[:],
+                    lhsT=codes[:, cols].bitcast(FP8X4),
+                    lhsT_scale=scales[:, cols],
+                    rhs=r_codes[nb][:, g, :].bitcast(FP4X4),
+                    rhs_scale=r_scales[:, g, nb * PASS:(nb + 1) * PASS],
+                    start=(g == 0), stop=(g == FG - 1),
+                )
+            return bank
+
+        def scale_add(i, nb, bank):
+            part = work.tile([P, PASS], F32, name="z_part")
+            nc.vector.scalar_tensor_tensor(
+                out=part[:], in0=bank[:], scalar=ss_col[:, i:i + 1], in1=other_all[:, nb * PASS:(nb + 1) * PASS],
+                op0=ALU.mult, op1=ALU.add,
+            )
+            return part
+
+        def gear(i, nb, part, eng):
+            if nb == 0:
+                y_f32[i] = work.tile([P, N], F32, name="y_f32")
+            cols = slice(nb * PASS, (nb + 1) * PASS)
+            eng.tensor_tensor(out=y_f32[i][:, cols], in0=part[:], in1=gear_all[:, cols], op=ALU.mult)
+
+        def store_y(i, cols):
+            nc.sync.dma_start(out=out_0[i * P:(i + 1) * P, cols], in_=y_f32[i][:, cols])
+
+        def round_y(i, nb):
+            rows = work.tile([P, PASS], BF16, name="y_rows%d" % nb, align_bytes=64)
+            nc.scalar.copy(
+                out=rows[:].rearrange("s (u j e) -> s u j e", u=2, e=2),
+                in_=y_f32[i][:, nb * PASS:(nb + 1) * PASS].rearrange("s (j u e) -> s u j e", u=2, e=2),
+            )
+            y_rows[(i, nb)] = rows
+
+        def gear_rounded(i, nb, part):
+            rows = work.tile([P, PASS], BF16, name="y_rows%d" % nb, align_bytes=64)
+            nc.vector.tensor_tensor(
+                out=rows[:].rearrange("s (u j e) -> s u j e", u=2, e=2),
+                in0=part[:].rearrange("s (j u e) -> s u j e", u=2, e=2),
+                in1=gear_all[:, nb * PASS:(nb + 1) * PASS].rearrange("s (j u e) -> s u j e", u=2, e=2),
+                op=ALU.mult,
+            )
+            y_rows[(i, nb)] = rows
+
+        y_codes = {}
+
+        def quantize_y(i, g):
+            if g == 0:
+                y_codes[i] = work.tile([P, NG, P], U32, name="y_codes", align_bytes=64)
+            nc.vector.quantize_mx(
+                out=y_codes[i][:, g, :].bitcast(FP8X4),
+                scales=y_scales[:, g, i * P:(i + 1) * P],
+                in_=y_turned[(i, g)],
+            )
+            if g == NG - 1:
+                dest = out_1.rearrange("g p m t -> p g (m t)").bitcast(I32)
+                nc.sync.dma_start(out=dest[:, :, i * P:(i + 1) * P], in_=y_codes[i][:].bitcast(I32))
+
+        def turn_half(words, name, copy):
+            bank = tp_bank()
+            for u in range(2):
+                nc.tensor.transpose(bank[:, u, :], words[u], ident[:])
+            turned = work.tile([P, PASS], BF16, name=name, align_bytes=64)
+            copy(out=turned[:].bitcast(F32).rearrange("p (s u) -> p s u", u=2), in_=bank[:, 0:2, :].rearrange("p u s -> p s u"))
+            return turned
+
+        def quantize_d(i):
+            codes, scales = quantize(d_turned[i], "d")
+            for g in range(KG):
+                d_q[(i, g)] = (codes[:, g * P:(g + 1) * P], scales[:, g * P:(g + 1) * P])
+
+        def quantize_h(i, h):
+            h_q[(i, h)] = quantize(h_turned[(i, h)], "h%d" % h)
+
+        def turn_h(i):
+            return [turn_pair(h_rows[(i, 2 * h)], h_rows[(i, 2 * h + 1)]) for h in range(2)]
+
+        def leave_h(i, banks):
+            for h in range(2):
+                h_turned[(i, h)] = leave_bank(banks[h], "h_turned%d" % h)
+
+        def turn_y(i):
+            return turn_pair(y_rows[(i, 0)], y_rows[(i, 1)])
+
+        def leave_y(i, bank):
+            turned = leave_bank(bank, "y_turned")
+            for g in range(NG):
+                y_turned[(i, g)] = turned[:, g * PASS:(g + 1) * PASS]
+
+        def live(i):
+            return 0 <= i < TILES
+
+        halves = []
+        for g in range(KG):
+            words = d_first[g][:].bitcast(F32)
+            copy = nc.vector.tensor_copy if g == 0 else nc.scalar.copy
+            halves.append(turn_half([words[:, u:256:2] for u in range(2)], "d_half", copy))
+        for g in range(KG):
+            codes = keep.tile([P, P], U32, name="d_first_codes%d" % g, align_bytes=64)
+            scales = keep.tile([P, P], U8, name="d_first_scales%d" % g, align_bytes=64)
+            nc.vector.quantize_mx(out=codes[:].bitcast(FP8X4), scales=scales[:], in_=halves[g][:])
+            d_q[(0, g)] = (codes[:], scales[:])
+        spread_cap()
+
+        last = TILES - 1
+        for j in range(last):
+            if live(j - 1):
+                quantize_h(j - 1, 1)
+            if live(j - 2):
+                for nb in range(NG):
+                    round_y(j - 2, nb)
+            if live(j + 2):
+                sort_d(j + 2)
+            mm1(j, 0)
+            mm1(j, 1)
+            if j == 0:
+                d_turned[1] = leave_bank(turn_d(1), "d_turned")
+            else:
+                quantize_d(j + 1)
+                gear(j - 1, 0, scale_add(j - 1, 0, mm2(j - 1, 0)), nc.gpsimd)
+            mm1(j, 2)
+            mm1(j, 3)
+            if j == 0:
+                quantize_d(1)
+                spread_row(other_col, other_all)
+                spread_row(gear_col, gear_all)
+                turn_ss()
+            else:
+                if live(j - 3):
+                    quantize_y(j - 3, 0)
+                part = scale_add(j - 1, 1, mm2(j - 1, 1))
+                if live(j - 3):
+                    quantize_y(j - 3, 1)
+                gear(j - 1, 1, part, nc.vector)
+                store_y(j - 1, slice(0, N))
+            h_banks = turn_h(j)
+            d_bank = turn_d(j + 2) if live(j + 2) else None
+            y_bank = turn_y(j - 2) if live(j - 2) else None
+            leave_h(j, h_banks)
+            quantize_h(j, 0)
+            if live(j + 2):
+                d_turned[j + 2] = leave_bank(d_bank, "d_turned")
+            if live(j - 2):
+                leave_y(j - 2, y_bank)
+
+        quantize_h(last - 1, 1)
+        for nb in range(NG):
+            round_y(last - 2, nb)
+        for fb in range(FG):
+            mm1(last, fb)
+        for g in range(NG):
+            quantize_y(last - 3, g)
+        gear(last - 1, 0, scale_add(last - 1, 0, mm2(last - 1, 0)), nc.vector)
+        h_banks = turn_h(last)
+        y_bank = turn_y(last - 2)
+        leave_h(last, h_banks)
+        leave_y(last - 2, y_bank)
+        round_y(last - 1, 0)
+        for h in range(2):
+            quantize_h(last, h)
+        for g in range(NG):
+            quantize_y(last - 2, g)
+        gear(last - 1, 1, scale_add(last - 1, 1, mm2(last - 1, 1)), nc.vector)
+        store_y(last - 1, slice(0, N))
+        round_y(last - 1, 1)
+        gear(last, 0, scale_add(last, 0, mm2(last, 0)), nc.gpsimd)
+        store_y(last, slice(0, PASS))
+        part = scale_add(last, 1, mm2(last, 1))
+        leave_y(last - 1, turn_y(last - 1))
+        round_y(last, 0)
+        gear_rounded(last, 1, part)
+        gear(last, 1, part, nc.vector)
+        store_y(last, slice(PASS, N))
+        for g in range(NG):
+            quantize_y(last - 1, g)
+        for g in (1, 0):
+            words = y_rows[(last, g)][:].bitcast(F32)
+            y_turned[(last, g)] = turn_half([words[:, u * P:(u + 1) * P] for u in range(2)], "y_half", nc.scalar.copy)[:]
+        for g in range(NG):
+            quantize_y(last, g)
+
+        dest = out_2.bitcast(I32)
+        for q in range(4):
+            eng = nc.sync if q % 2 == 0 else nc.scalar
+            eng.dma_start(
+                out=dest[:, 4 * q:4 * q + 4, :].rearrange("g r c -> r g c"),
+                in_=y_scales[32 * q:32 * q + 4, :, :].bitcast(I32),
+            )

@@ -45,7 +45,7 @@ def tile_capped_interbank_loss_planes_h1_kernel(
             used.append("tp")
             return psum.tile([P, 4, P], F32, name="tp%d" % (n % RING))
 
-        c_scales = keep.tile([P, KG, F], U8, align_bytes=64)
+        c_scales = [keep.tile([P, KG, F // 2], U8, name="c_scales%d" % h, align_bytes=64) for h in range(2)]
         r_scales = keep.tile([P, FG, N], U8, align_bytes=64)
         ident = keep.tile([P, P], F32)
 
@@ -62,8 +62,7 @@ def tile_capped_interbank_loss_planes_h1_kernel(
         def load_d(i):
             nc.sync.dma_start(out=d_raw[i][:], in_=default_grades[i * P:(i + 1) * P, :])
 
-        def load_scales(plane, scales):
-            words = scales.bitcast(I32)
+        def load_scales(plane, words):
             for q in range(4):
                 nc.sync.dma_start(
                     out=plane[32 * q:32 * q + 4, :, :].bitcast(I32),
@@ -74,24 +73,26 @@ def tile_capped_interbank_loss_planes_h1_kernel(
             words = words.bitcast(I32).rearrange("g p c -> p g c")
             nc.sync.dma_start(out=tile[:].bitcast(I32), in_=words[:, :, b * 256:(b + 1) * 256])
 
-        nc.vector.memset(c_scales[:].bitcast(I32), 0)
+        nc.gpsimd.memset(c_scales[0][:].bitcast(I32), 0)
+        nc.vector.memset(c_scales[1][:].bitcast(I32), 0)
         nc.vector.memset(r_scales[:].bitcast(I32), 0)
         nc.vector.memset(ss_stage[:], 0.0)
-        nc.gpsimd.dma_start(out=cap_col[:], in_=loss_cap.rearrange("(p c) -> p c", p=P))
         make_identity(nc, ident[:])
         nc.gpsimd.dma_start(out=other_col[:], in_=other_result.rearrange("(p c) -> p c", p=P))
         nc.gpsimd.dma_start(out=gear_col[:], in_=gearing.rearrange("(p c) -> p c", p=P))
         nc.gpsimd.dma_start(out=ss_rows[:], in_=scenario_scale.rearrange("(i p) -> i p", p=P))
         for g in range(KG):
             nc.sync.dma_start(out=d_first[g][:], in_=default_grades[0:P, g * PASS:(g + 1) * PASS])
+        nc.sync.dma_start(out=cap_col[:], in_=loss_cap.rearrange("(p c) -> p c", p=P))
+        load_scales(c_scales[0], claims_scales.bitcast(I32)[:, :, 0:256])
         load_codes(c_codes[0], claims_words, 0)
-        load_scales(c_scales, claims_scales)
         load_codes(c_codes[1], claims_words, 1)
         load_d(1)
+        load_scales(c_scales[1], claims_scales.bitcast(I32)[:, :, 256:512])
         load_codes(c_codes[2], claims_words, 2)
         load_codes(c_codes[3], claims_words, 3)
         load_d(2)
-        load_scales(r_scales, recovery_scales)
+        load_scales(r_scales, recovery_scales.bitcast(I32))
         for nb in range(NG):
             load_codes(r_codes[nb], recovery_words, nb)
         for i in range(3, TILES):
@@ -101,7 +102,9 @@ def tile_capped_interbank_loss_planes_h1_kernel(
         other_all = keep.tile([P, N], BF16)
         gear_all = keep.tile([P, N], BF16)
         ss_col = keep.tile([P, TILES], F32)
-        y_scales = keep.tile([P, NG, S], U8, align_bytes=64)
+        early = 6
+        y_scales = [keep.tile([P, NG, early * P], U8, name="y_scales_early", align_bytes=64),
+                    keep.tile([P, NG, S - early * P], U8, name="y_scales_late", align_bytes=64)]
 
         def spread_cap():
             words = cap_col[:].bitcast(F32)
@@ -173,7 +176,7 @@ def tile_capped_interbank_loss_planes_h1_kernel(
                     lhsT=codes.bitcast(FP8X4),
                     lhsT_scale=scales,
                     rhs=c_codes[fb][:, g, :].bitcast(FP4X4),
-                    rhs_scale=c_scales[:, g, fb * PASS:(fb + 1) * PASS],
+                    rhs_scale=c_scales[fb // 2][:, g, (fb % 2) * PASS:(fb % 2 + 1) * PASS],
                     start=(g == 0), stop=(g == KG - 1),
                 )
             rows = work.tile([P, PASS], BF16, name="h_rows%d" % fb, align_bytes=64)
@@ -249,7 +252,7 @@ def tile_capped_interbank_loss_planes_h1_kernel(
                 y_codes[i] = work.tile([P, NG, P], U32, name="y_codes", align_bytes=64)
             nc.vector.quantize_mx(
                 out=y_codes[i][:, g, :].bitcast(FP8X4),
-                scales=y_scales[:, g, i * P:(i + 1) * P],
+                scales=y_scales[i // early][:, g, (i % early) * P:(i % early + 1) * P],
                 in_=y_turned[(i, g)],
             )
             if g == NG - 1:
@@ -302,37 +305,49 @@ def tile_capped_interbank_loss_planes_h1_kernel(
             d_q[(0, g)] = (codes[:], scales[:])
         spread_cap()
 
+        def store_scales(part, cols, engines):
+            dest = out_2.bitcast(I32)[:, :, cols]
+            for q in range(4):
+                engines[q % len(engines)].dma_start(
+                    out=dest[:, 4 * q:4 * q + 4, :].rearrange("g r c -> r g c"),
+                    in_=y_scales[part][32 * q:32 * q + 4, :, :].bitcast(I32),
+                )
+
         last = TILES - 1
+        z_bank = {}
+
+        def finish_second_half(i):
+            gear(i, 1, scale_add(i, 1, z_bank[i]), nc.gpsimd)
+            store_y(i, slice(0, N))
+
         for j in range(last):
             if live(j - 1):
                 quantize_h(j - 1, 1)
             if live(j - 2):
-                for nb in range(NG):
-                    round_y(j - 2, nb)
+                round_y(j - 2, 0)
+                finish_second_half(j - 2)
             if live(j + 2):
                 sort_d(j + 2)
+            if live(j - 2):
+                round_y(j - 2, 1)
             mm1(j, 0)
             mm1(j, 1)
             if j == 0:
                 d_turned[1] = leave_bank(turn_d(1), "d_turned")
             else:
-                quantize_d(j + 1)
                 gear(j - 1, 0, scale_add(j - 1, 0, mm2(j - 1, 0)), nc.gpsimd)
             mm1(j, 2)
             mm1(j, 3)
+            quantize_d(j + 1)
             if j == 0:
-                quantize_d(1)
                 spread_row(other_col, other_all)
                 spread_row(gear_col, gear_all)
                 turn_ss()
             else:
-                if live(j - 3):
-                    quantize_y(j - 3, 0)
-                part = scale_add(j - 1, 1, mm2(j - 1, 1))
-                if live(j - 3):
-                    quantize_y(j - 3, 1)
-                gear(j - 1, 1, part, nc.vector)
-                store_y(j - 1, slice(0, N))
+                z_bank[j - 1] = mm2(j - 1, 1)
+            if live(j - 3):
+                for g in range(NG):
+                    quantize_y(j - 3, g)
             h_banks = turn_h(j)
             d_bank = turn_d(j + 2) if live(j + 2) else None
             y_bank = turn_y(j - 2) if live(j - 2) else None
@@ -344,8 +359,9 @@ def tile_capped_interbank_loss_planes_h1_kernel(
                 leave_y(j - 2, y_bank)
 
         quantize_h(last - 1, 1)
-        for nb in range(NG):
-            round_y(last - 2, nb)
+        round_y(last - 2, 0)
+        finish_second_half(last - 2)
+        round_y(last - 2, 1)
         for fb in range(FG):
             mm1(last, fb)
         for g in range(NG):
@@ -361,6 +377,7 @@ def tile_capped_interbank_loss_planes_h1_kernel(
         for g in range(NG):
             quantize_y(last - 2, g)
         gear(last - 1, 1, scale_add(last - 1, 1, mm2(last - 1, 1)), nc.vector)
+        store_scales(0, slice(0, early * 32), [nc.sync])
         store_y(last - 1, slice(0, N))
         round_y(last - 1, 1)
         gear(last, 0, scale_add(last, 0, mm2(last, 0)), nc.gpsimd)
@@ -369,20 +386,13 @@ def tile_capped_interbank_loss_planes_h1_kernel(
         leave_y(last - 1, turn_y(last - 1))
         round_y(last, 0)
         gear_rounded(last, 1, part)
-        gear(last, 1, part, nc.vector)
-        store_y(last, slice(PASS, N))
         for g in range(NG):
             quantize_y(last - 1, g)
+        gear(last, 1, part, nc.vector)
+        store_y(last, slice(PASS, N))
         for g in (1, 0):
             words = y_rows[(last, g)][:].bitcast(F32)
             y_turned[(last, g)] = turn_half([words[:, u * P:(u + 1) * P] for u in range(2)], "y_half", nc.scalar.copy)[:]
         for g in range(NG):
             quantize_y(last, g)
-
-        dest = out_2.bitcast(I32)
-        for q in range(4):
-            eng = nc.sync if q % 2 == 0 else nc.scalar
-            eng.dma_start(
-                out=dest[:, 4 * q:4 * q + 4, :].rearrange("g r c -> r g c"),
-                in_=y_scales[32 * q:32 * q + 4, :, :].bitcast(I32),
-            )
+        store_scales(1, slice(early * 32, S // 4), [nc.scalar, nc.sync])

from contextlib import ExitStack

import concourse.mybir as mybir
from concourse.masks import make_identity

S, K, F, N = 1024, 1024, 2048, 1024
FLOPS = 2 * S * K * F + 2 * S * F * N

F32 = mybir.dt.float32
BF16 = mybir.dt.bfloat16
I32 = mybir.dt.int32
U32 = mybir.dt.uint32
U8 = mybir.dt.uint8
FP8X4 = mybir.dt.float8_e4m3fn_x4
FP4X4 = mybir.dt.float4_e2m1fn_x4
ALU = mybir.AluOpType

P = 128
PASS = 512
TILES = S // P
KG, FG, NG = K // PASS, F // PASS, N // PASS
RING = 4


def tile_capped_interbank_loss_planes_h1_kernel(
    tc, default_grades, claims_words, claims_scales, loss_cap, recovery_words, recovery_scales,
    scenario_scale, other_result, gearing, out_0, out_1, out_2,
):
    nc = tc.nc
    with ExitStack() as ctx:
        keep = ctx.enter_context(tc.tile_pool(name="keep", bufs=1))
        work = ctx.enter_context(tc.tile_pool(name="work", bufs=3))
        psum = ctx.enter_context(tc.psum_pool(name="psum", bufs=1))
        ctx.enter_context(tc.manual_schedule())

        used = []

        def mm_bank():
            n = len([x for x in used if x == "mm"])
            used.append("mm")
            return psum.tile([P, PASS], F32, name="mm%d" % (n % RING))

        def tp_bank():
            n = len([x for x in used if x == "tp"])
            used.append("tp")
            return psum.tile([P, 4, P], F32, name="tp%d" % (n % RING))

        c_scales = [keep.tile([P, KG, F // 2], U8, name="c_scales%d" % h, align_bytes=64) for h in range(2)]
        r_scales = keep.tile([P, FG, N], U8, align_bytes=64)
        ident = keep.tile([P, P], F32)

        d_raw = [None] + [keep.tile([P, K], BF16, name="d_raw%d" % i, align_bytes=64) for i in range(1, TILES)]
        c_codes = [keep.tile([P, KG, 2 * PASS], U8, name="c_codes%d" % fb, align_bytes=64) for fb in range(FG)]
        r_codes = [keep.tile([P, FG, 2 * PASS], U8, name="r_codes%d" % nb, align_bytes=64) for nb in range(NG)]
        d_first = [keep.tile([P, PASS], BF16, name="d_first%d" % g, align_bytes=64) for g in range(KG)]
        cap_col = keep.tile([P, 16], BF16)
        other_col = keep.tile([P, 8], BF16)
        gear_col = keep.tile([P, 8], BF16)
        ss_rows = keep.tile([TILES, P], BF16)
        ss_stage = keep.tile([P, P], F32)

        def load_d(i):
            nc.sync.dma_start(out=d_raw[i][:], in_=default_grades[i * P:(i + 1) * P, :])

        def load_scales(plane, words):
            for q in range(4):
                nc.sync.dma_start(
                    out=plane[32 * q:32 * q + 4, :, :].bitcast(I32),
                    in_=words[:, 4 * q:4 * q + 4, :].rearrange("g r c -> r g c"),
                )

        def load_codes(tile, words, b):
            words = words.bitcast(I32).rearrange("g p c -> p g c")
            nc.sync.dma_start(out=tile[:].bitcast(I32), in_=words[:, :, b * 256:(b + 1) * 256])

        nc.gpsimd.memset(c_scales[0][:].bitcast(I32), 0)
        nc.vector.memset(c_scales[1][:].bitcast(I32), 0)
        nc.vector.memset(r_scales[:].bitcast(I32), 0)
        nc.vector.memset(ss_stage[:], 0.0)
        make_identity(nc, ident[:])
        nc.gpsimd.dma_start(out=other_col[:], in_=other_result.rearrange("(p c) -> p c", p=P))
        nc.gpsimd.dma_start(out=gear_col[:], in_=gearing.rearrange("(p c) -> p c", p=P))
        nc.gpsimd.dma_start(out=ss_rows[:], in_=scenario_scale.rearrange("(i p) -> i p", p=P))
        for g in range(KG):
            nc.sync.dma_start(out=d_first[g][:], in_=default_grades[0:P, g * PASS:(g + 1) * PASS])
        nc.sync.dma_start(out=cap_col[:], in_=loss_cap.rearrange("(p c) -> p c", p=P))
        load_scales(c_scales[0], claims_scales.bitcast(I32)[:, :, 0:256])
        load_codes(c_codes[0], claims_words, 0)
        load_codes(c_codes[1], claims_words, 1)
        load_d(1)
        load_scales(c_scales[1], claims_scales.bitcast(I32)[:, :, 256:512])
        load_codes(c_codes[2], claims_words, 2)
        load_codes(c_codes[3], claims_words, 3)
        load_d(2)
        load_scales(r_scales, recovery_scales.bitcast(I32))
        for nb in range(NG):
            load_codes(r_codes[nb], recovery_words, nb)
        for i in range(3, TILES):
            load_d(i)

        cap_all = keep.tile([P, FG, PASS], BF16)
        other_all = keep.tile([P, N], BF16)
        gear_all = keep.tile([P, N], BF16)
        ss_col = keep.tile([P, TILES], F32)
        early = 6
        y_scales = [keep.tile([P, NG, early * P], U8, name="y_scales_early", align_bytes=64),
                    keep.tile([P, NG, S - early * P], U8, name="y_scales_late", align_bytes=64)]

        def spread_cap():
            words = cap_col[:].bitcast(F32)
            dest = cap_all[:].bitcast(F32).rearrange("m g (u h l) -> m g u h l", u=2, l=4)
            for u in range(2):
                bank = tp_bank()
                for l in range(4):
                    c = 2 * l + u
                    nc.tensor.transpose(bank[:, l, :], words[:, c:c + 1].to_broadcast([P, P]), ident[:])
                copy = nc.vector.tensor_copy if u == 0 else nc.scalar.copy
                copy(out=dest[:, :, u, :, :], in_=bank[:].rearrange("m l (g h) -> m g h l", g=FG))

        def spread_row(col, dest):
            words = col[:].bitcast(F32)
            bank = tp_bank()
            for c in range(4):
                nc.tensor.transpose(bank[:, c, :], words[:, c:c + 1].to_broadcast([P, P]), ident[:])
            nc.scalar.copy(out=dest[:].bitcast(F32).rearrange("m (p c) -> m p c", c=4), in_=bank[:].rearrange("m c p -> m p c"))

        def turn_ss():
            nc.scalar.copy(out=ss_stage[0:TILES, :], in_=ss_rows[:])
            bank = tp_bank()
            nc.tensor.transpose(bank[:, 0, :], ss_stage[:], ident[:])
            nc.scalar.copy(out=ss_col[:], in_=bank[:, 0, 0:TILES])

        d_sorted, d_turned, d_q = {}, {}, {}
        h_rows, h_turned, h_q = {}, {}, {}
        z_part, y_f32, y_rows, y_turned = {}, {}, {}, {}

        def leave_bank(bank, name):
            turned = work.tile([P, 1024], BF16, name=name, align_bytes=64)
            nc.scalar.copy(
                out=turned[:].bitcast(F32).rearrange("p (g s u) -> p g s u", g=2, u=2),
                in_=bank[:].rearrange("p (g u) s -> p g s u", u=2),
            )
            return turned

        def sort_d(i):
            srt = work.tile([P, K // 2], F32, name="d_sorted")
            nc.scalar.copy(
                out=srt[:].rearrange("s (g u j) -> s g u j", g=KG, u=2),
                in_=d_raw[i][:].bitcast(F32).rearrange("s (g j u) -> s g u j", g=KG, u=2),
            )
            d_sorted[i] = srt

        def turn_d(i):
            bank = tp_bank()
            for g in range(KG):
                for u in range(2):
                    if i in d_sorted:
                        src = d_sorted[i][:, (2 * g + u) * P:(2 * g + u + 1) * P]
                    else:
                        src = d_raw[i][:].bitcast(F32)[:, 256 * g + u:256 * (g + 1):2]
                    nc.tensor.transpose(bank[:, 2 * g + u, :], src, ident[:])
            return bank

        def quantize(turned, name):
            codes = work.tile([P, 256], U32, name=name + "_codes", align_bytes=64)
            scales = work.tile([P, 256], U8, name=name + "_scales", align_bytes=64)
            nc.vector.quantize_mx(out=codes[:].bitcast(FP8X4), scales=scales[:], in_=turned[:])
            return codes, scales

        def mm1(i, fb):
            bank = mm_bank()
            for g in range(KG):
                codes, scales = d_q[(i, g)]
                nc.tensor.matmul_mx(
                    out=bank[:],
                    lhsT=codes.bitcast(FP8X4),
                    lhsT_scale=scales,
                    rhs=c_codes[fb][:, g, :].bitcast(FP4X4),
                    rhs_scale=c_scales[fb // 2][:, g, (fb % 2) * PASS:(fb % 2 + 1) * PASS],
                    start=(g == 0), stop=(g == KG - 1),
                )
            rows = work.tile([P, PASS], BF16, name="h_rows%d" % fb, align_bytes=64)
            nc.vector.tensor_tensor(
                out=rows[:].rearrange("s (u j e) -> s u j e", u=2, e=2),
                in0=bank[:].rearrange("s (j u e) -> s u j e", u=2, e=2),
                in1=cap_all[:, fb, :].rearrange("s (u j e) -> s u j e", u=2, e=2),
                op=ALU.min,
            )
            h_rows[(i, fb)] = rows

        def turn_pair(rows_a, rows_b):
            bank = tp_bank()
            for g, rows in enumerate((rows_a, rows_b)):
                for u in range(2):
                    nc.tensor.transpose(bank[:, 2 * g + u, :], rows[:].bitcast(F32)[:, u * P:(u + 1) * P], ident[:])
            return bank

        def mm2(i, nb):
            bank = mm_bank()
            for g in range(FG):
                codes, scales = h_q[(i, g // 2)]
                cols = slice((g % 2) * P, (g % 2 + 1) * P)
                nc.tensor.matmul_mx(
                    out=bank[:],
                    lhsT=codes[:, cols].bitcast(FP8X4),
                    lhsT_scale=scales[:, cols],
                    rhs=r_codes[nb][:, g, :].bitcast(FP4X4),
                    rhs_scale=r_scales[:, g, nb * PASS:(nb + 1) * PASS],
                    start=(g == 0), stop=(g == FG - 1),
                )
            return bank

        def scale_add(i, nb, bank):
            part = work.tile([P, PASS], F32, name="z_part")
            nc.vector.scalar_tensor_tensor(
                out=part[:], in0=bank[:], scalar=ss_col[:, i:i + 1], in1=other_all[:, nb * PASS:(nb + 1) * PASS],
                op0=ALU.mult, op1=ALU.add,
            )
            return part

        def gear(i, nb, part, eng):
            if nb == 0:
                y_f32[i] = work.tile([P, N], F32, name="y_f32")
            cols = slice(nb * PASS, (nb + 1) * PASS)
            eng.tensor_tensor(out=y_f32[i][:, cols], in0=part[:], in1=gear_all[:, cols], op=ALU.mult)

        def store_y(i, cols):
            nc.sync.dma_start(out=out_0[i * P:(i + 1) * P, cols], in_=y_f32[i][:, cols])

        def round_y(i, nb):
            rows = work.tile([P, PASS], BF16, name="y_rows%d" % nb, align_bytes=64)
            nc.scalar.copy(
                out=rows[:].rearrange("s (u j e) -> s u j e", u=2, e=2),
                in_=y_f32[i][:, nb * PASS:(nb + 1) * PASS].rearrange("s (j u e) -> s u j e", u=2, e=2),
            )
            y_rows[(i, nb)] = rows

        def gear_rounded(i, nb, part):
            rows = work.tile([P, PASS], BF16, name="y_rows%d" % nb, align_bytes=64)
            nc.vector.tensor_tensor(
                out=rows[:].rearrange("s (u j e) -> s u j e", u=2, e=2),
                in0=part[:].rearrange("s (j u e) -> s u j e", u=2, e=2),
                in1=gear_all[:, nb * PASS:(nb + 1) * PASS].rearrange("s (j u e) -> s u j e", u=2, e=2),
                op=ALU.mult,
            )
            y_rows[(i, nb)] = rows

        y_codes = {}

        def quantize_y(i, g):
            if g == 0:
                y_codes[i] = work.tile([P, NG, P], U32, name="y_codes", align_bytes=64)
            nc.vector.quantize_mx(
                out=y_codes[i][:, g, :].bitcast(FP8X4),
                scales=y_scales[i // early][:, g, (i % early) * P:(i % early + 1) * P],
                in_=y_turned[(i, g)],
            )
            if g == NG - 1:
                dest = out_1.rearrange("g p m t -> p g (m t)").bitcast(I32)
                nc.sync.dma_start(out=dest[:, :, i * P:(i + 1) * P], in_=y_codes[i][:].bitcast(I32))

        def turn_half(words, name, copy):
            bank = tp_bank()
            for u in range(2):
                nc.tensor.transpose(bank[:, u, :], words[u], ident[:])
            turned = work.tile([P, PASS], BF16, name=name, align_bytes=64)
            copy(out=turned[:].bitcast(F32).rearrange("p (s u) -> p s u", u=2), in_=bank[:, 0:2, :].rearrange("p u s -> p s u"))
            return turned

        def quantize_d(i):
            codes, scales = quantize(d_turned[i], "d")
            for g in range(KG):
                d_q[(i, g)] = (codes[:, g * P:(g + 1) * P], scales[:, g * P:(g + 1) * P])

        def quantize_h(i, h):
            h_q[(i, h)] = quantize(h_turned[(i, h)], "h%d" % h)

        def turn_h(i):
            return [turn_pair(h_rows[(i, 2 * h)], h_rows[(i, 2 * h + 1)]) for h in range(2)]

        def leave_h(i, banks):
            for h in range(2):
                h_turned[(i, h)] = leave_bank(banks[h], "h_turned%d" % h)

        def turn_y(i):
            return turn_pair(y_rows[(i, 0)], y_rows[(i, 1)])

        def leave_y(i, bank):
            turned = leave_bank(bank, "y_turned")
            for g in range(NG):
                y_turned[(i, g)] = turned[:, g * PASS:(g + 1) * PASS]

        def live(i):
            return 0 <= i < TILES

        halves = []
        for g in range(KG):
            words = d_first[g][:].bitcast(F32)
            copy = nc.vector.tensor_copy if g == 0 else nc.scalar.copy
            halves.append(turn_half([words[:, u:256:2] for u in range(2)], "d_half", copy))
        for g in range(KG):
            codes = keep.tile([P, P], U32, name="d_first_codes%d" % g, align_bytes=64)
            scales = keep.tile([P, P], U8, name="d_first_scales%d" % g, align_bytes=64)
            nc.vector.quantize_mx(out=codes[:].bitcast(FP8X4), scales=scales[:], in_=halves[g][:])
            d_q[(0, g)] = (codes[:], scales[:])
        spread_cap()

        def store_scales(part, cols, engines):
            dest = out_2.bitcast(I32)[:, :, cols]
            for q in range(4):
                engines[q % len(engines)].dma_start(
                    out=dest[:, 4 * q:4 * q + 4, :].rearrange("g r c -> r g c"),
                    in_=y_scales[part][32 * q:32 * q + 4, :, :].bitcast(I32),
                )

        last = TILES - 1
        z_bank = {}

        def finish_second_half(i):
            gear(i, 1, scale_add(i, 1, z_bank[i]), nc.gpsimd)
            store_y(i, slice(0, N))

        for j in range(last):
            if live(j - 1):
                quantize_h(j - 1, 1)
            if live(j - 2):
                round_y(j - 2, 0)
                finish_second_half(j - 2)
            if live(j + 2):
                sort_d(j + 2)
            if live(j - 2):
                round_y(j - 2, 1)
            mm1(j, 0)
            mm1(j, 1)
            if j == 0:
                d_turned[1] = leave_bank(turn_d(1), "d_turned")
            else:
                gear(j - 1, 0, scale_add(j - 1, 0, mm2(j - 1, 0)), nc.gpsimd)
            mm1(j, 2)
            mm1(j, 3)
            quantize_d(j + 1)
            if j == 0:
                spread_row(other_col, other_all)
                spread_row(gear_col, gear_all)
                turn_ss()
            else:
                z_bank[j - 1] = mm2(j - 1, 1)
            if live(j - 3):
                for g in range(NG):
                    quantize_y(j - 3, g)
            h_banks = turn_h(j)
            d_bank = turn_d(j + 2) if live(j + 2) else None
            y_bank = turn_y(j - 2) if live(j - 2) else None
            leave_h(j, h_banks)
            quantize_h(j, 0)
            if live(j + 2):
                d_turned[j + 2] = leave_bank(d_bank, "d_turned")
            if live(j - 2):
                leave_y(j - 2, y_bank)

        quantize_h(last - 1, 1)
        round_y(last - 2, 0)
        finish_second_half(last - 2)
        round_y(last - 2, 1)
        for fb in range(FG):
            mm1(last, fb)
        for g in range(NG):
            quantize_y(last - 3, g)
        gear(last - 1, 0, scale_add(last - 1, 0, mm2(last - 1, 0)), nc.vector)
        h_banks = turn_h(last)
        y_bank = turn_y(last - 2)
        leave_h(last, h_banks)
        leave_y(last - 2, y_bank)
        round_y(last - 1, 0)
        for h in range(2):
            quantize_h(last, h)
        for g in range(NG):
            quantize_y(last - 2, g)
        gear(last - 1, 1, scale_add(last - 1, 1, mm2(last - 1, 1)), nc.vector)
        store_scales(0, slice(0, early * 32), [nc.sync])
        store_y(last - 1, slice(0, N))
        round_y(last - 1, 1)
        gear(last, 0, scale_add(last, 0, mm2(last, 0)), nc.gpsimd)
        store_y(last, slice(0, PASS))
        part = scale_add(last, 1, mm2(last, 1))
        leave_y(last - 1, turn_y(last - 1))
        round_y(last, 0)
        gear_rounded(last, 1, part)
        for g in range(NG):
            quantize_y(last - 1, g)
        gear(last, 1, part, nc.vector)
        store_y(last, slice(PASS, N))
        for g in (1, 0):
            words = y_rows[(last, g)][:].bitcast(F32)
            y_turned[(last, g)] = turn_half([words[:, u * P:(u + 1) * P] for u in range(2)], "y_half", nc.scalar.copy)[:]
        for g in range(NG):
            quantize_y(last, g)
        store_scales(1, slice(early * 32, S // 4), [nc.scalar, nc.sync])
